import numpy as np
import ml_dtypes


def mxq(x, axis, fmt="e4m3"):
    dtype, down = {"e4m3": (ml_dtypes.float8_e4m3fn, 7), "e5m2": (ml_dtypes.float8_e5m2, 14)}[fmt]
    v = np.moveaxis(np.asarray(x, np.float32).astype(ml_dtypes.bfloat16).astype(np.float64), axis, -1)
    blocks = v.reshape(v.shape[:-1] + (-1, 32))
    amax = np.abs(blocks).max(-1, keepdims=True)
    byte = np.maximum(np.where(amax > 0, np.frexp(amax)[1] - 1 + 127, 0) - down, 1)
    scale = np.exp2(byte - 127.0)
    codes = (blocks / scale).astype(np.float32).astype(dtype).astype(np.float64)
    return np.moveaxis((codes * scale).reshape(v.shape), -1, axis)


WIDE = False


def mx_kscale(k):
    if not WIDE:
        return np.ones(k)
    levels = np.array([10, -10, 5, -5, 0])
    if k % 512:
        return np.exp2(np.random.permutation(np.resize(levels, k // 32))).repeat(32)
    a = np.empty((k // 512, 16))
    for p in range(k // 512):
        a[p, :8] = np.random.permutation(np.resize(levels, 8))
        for g in range(8):
            far = levels[np.abs(levels - a[p, g]) >= 10]
            a[p, g + 8] = far[np.random.randint(len(far))]
    return np.exp2(a.ravel()).repeat(32)


def f64(x):
    return np.asarray(x).astype(np.float64)


def striped(idx):
    return np.tile(idx.reshape(-1, 16).T, (8, 1)).astype(np.uint16)


def unstriped(offs):
    return offs[:16].T.reshape(-1).astype(np.int64)


def striped8(idx):
    return np.concatenate([x.reshape(-1, 16).T for x in idx]).astype(np.uint16)


def runs(offs, k):
    lists = np.stack([offs[16 * r : 16 * r + 16].T.reshape(-1) for r in range(8)]).astype(np.int64)
    return lists[np.arange(k) % 512 // 64]


def pack_weight(w):
    k, n = w.shape
    w = f64(np.asarray(w, np.float32).astype(ml_dtypes.bfloat16)).reshape(k // 32, 32, n)
    amax = np.abs(w).max(1)
    byte = np.clip(np.where(amax > 0, np.frexp(amax)[1] - 1 + 127 - 7, 1), 1, 254)
    scaled = (w * np.exp2(127.0 - byte)[:, None, :]).reshape(k, n).astype(np.float32)
    words = np.ascontiguousarray(scaled.reshape(k // 512, 128, 4, n).transpose(0, 1, 3, 2)).astype(ml_dtypes.float8_e4m3fn).view(np.uint8)
    return words, np.ascontiguousarray(byte.astype(np.uint8).reshape(k // 512, 16, n))


def unpack_weight(words, scales):
    g, p, n, _ = words.shape
    vals = np.ascontiguousarray(words).view(ml_dtypes.float8_e4m3fn).astype(np.float64) * np.repeat(np.exp2(scales.astype(np.float64) - 127.0), 8, axis=1)[..., None]
    return vals.transpose(0, 1, 3, 2).reshape(g * 512, n)


def sigmoid(v):
    return 1.0 / (1.0 + np.exp(-np.maximum(v, -700.0)))


K, T, S, G, H, W, U = 512, 2048, 256, 2048, 512, 128, 1024


def setup_inputs():
    n = np.random.standard_normal
    s = mx_kscale(K)[:, None]
    packed_xT = pack_weight(n((K, T)) * s)
    packed_dT = pack_weight(n((K, G)) / s)
    perm = np.random.permutation(S)
    return {
        "x_words": packed_xT[0],
        "x_scales": packed_xT[1],
        "d_words": packed_dT[0],
        "d_scales": packed_dT[1],
        "sl": np.random.uniform(1.0, 2.0, (H, 1)).astype(np.float32),
        "th": (0.5 * n((H, 1))).astype(np.float32),
        "gs": (np.random.uniform(0.5, 1.5, (K, 1)) * s).astype(np.float32),
        "mem": n((H, U)).astype(np.float32),
        "sl2": np.random.uniform(1.0, 2.0, (H, 1)).astype(np.float32),
        "th2": (0.5 * n((H, 1))).astype(np.float32),
        "offs": striped(np.random.permutation(T)[:S]),
        "k1": striped8(np.random.randint(0, G, (8, H))),
        "n1": striped(perm[:W]),
        "n2": striped(perm[W:]),
        "n3": striped(np.random.permutation(U)[:S]),
        "n4": striped(np.random.permutation(S)),
    }


def reference(x_words, x_scales, d_words, d_scales, sl, th, gs, mem, sl2, th2, offs, k1, n1, n2, n3, n4):
    old = f64(mem)[:, unstriped(n3)]
    d_k1 = unpack_weight(d_words, d_scales)[np.arange(K)[:, None], runs(k1, K)]
    xq = unpack_weight(x_words, x_scales)[:, unstriped(offs)]
    h = 0.0625 * (d_k1.T @ xq)
    pb = h[:, unstriped(n2)]
    sg = sigmoid(f64(sl) * (h[:, unstriped(n1)] - f64(th)))
    rb = pb - sg
    pa = h[:, unstriped(n1)]
    sg2 = sigmoid(f64(sl) * (h[:, unstriped(n2)] - f64(th)))
    ra = pa * sg2
    ds = np.zeros((H, S))
    ds[:, unstriped(n1)] = ra
    dt = ds.copy()
    dt[:, unstriped(n2)] = rb
    z = f64(gs) * dt
    h2 = 0.0625 * ((d_k1.T @ mxq(z, 0, "e4m3")))
    sg3 = sigmoid(f64(sl2) * (h2[:, unstriped(n4)] - f64(th2)))
    nw = old + sg3 * (h2 - old)
    out = f64(mem).copy()
    out[:, unstriped(n3)] = nw
    return out

@@ -1,0 +1,205 @@
+from contextlib import ExitStack
+
+import concourse.mybir as mybir
+
+K, T, S, G, H, W, U = 512, 2048, 256, 2048, 512, 128, 1024
+FLOPS = 2 * 2 * K * H * S
+
+F32 = mybir.dt.float32
+BF16 = mybir.dt.bfloat16
+I32 = mybir.dt.int32
+U32 = mybir.dt.uint32
+U16 = mybir.dt.uint16
+U8 = mybir.dt.uint8
+FP8X4 = mybir.dt.float8_e4m3fn_x4
+MULT = mybir.AluOpType.mult
+ADD = mybir.AluOpType.add
+SUB = mybir.AluOpType.subtract
+COPY = mybir.ActivationFunctionType.Copy
+SIGMOID = mybir.ActivationFunctionType.Sigmoid
+
+P = 128
+PACK = 4
+
+
+def tile_picked_ringeodepg_none_p_kernel(
+    tc, x_words, x_scales, d_words, d_scales, sl, th, gs, mem, sl2, th2, offs, k1, n1, n2, n3, n4, out
+):
+    nc = tc.nc
+    with ExitStack() as ctx:
+        lists = ctx.enter_context(tc.tile_pool(name="lists", bufs=1))
+        keep = ctx.enter_context(tc.tile_pool(name="keep", bufs=1))
+        big = ctx.enter_context(tc.tile_pool(name="big", bufs=1))
+        psum = ctx.enter_context(tc.psum_pool(name="psum", bufs=1))
+
+        def load_list(name, src):
+            tile = lists.tile(list(src.shape), U16, name=name)
+            nc.sync.dma_start(tile[:], src)
+            return tile
+
+        def load_words(name, src, offset):
+            tile = big.tile([P, T], U32, name=name, offset=offset)
+            nc.sync.dma_start(tile[:].bitcast(I32), src[0].rearrange("p c r -> p (c r)").bitcast(I32))
+            return tile
+
+        def load_rows(name, src):
+            tile = keep.tile([P, PACK], F32, name=name)
+            nc.gpsimd.dma_start(tile[:], src.rearrange("(p t) o -> p (t o)", t=PACK))
+            return tile
+
+        def minus_product(name, a, b):
+            prod = keep.tile([P, PACK], F32, name=name + "_pos")
+            nc.gpsimd.tensor_tensor(prod[:], a[:], b[:], MULT)
+            neg = keep.tile([P, PACK], F32, name=name)
+            nc.gpsimd.tensor_scalar(neg[:], prod[:], -1.0, 0.0, MULT, ADD)
+            return neg
+
+        k1_t = load_list("k1_t", k1)
+        d_scale_table = keep.tile([P, G], U8, name="d_scale_table")
+        nc.sync.dma_start(
+            d_scale_table[:].bitcast(I32),
+            d_scales[0].bitcast(I32).unsqueeze(1).to_broadcast([16, 8, G // 4]),
+        )
+        offs_t = load_list("offs_t", offs)
+        n1_t = load_list("n1_t", n1)
+        n2_t = load_list("n2_t", n2)
+        n4_t = load_list("n4_t", n4)
+        d_word_table = load_words("d_word_table", d_words, 0)
+        n3_t = load_list("n3_t", n3)
+        x_scale_table = keep.tile([P, T], U8, name="x_scale_table")
+        nc.vector.memset(x_scale_table[:].bitcast(I32), 0)
+        for q, queue in enumerate((nc.gpsimd, nc.gpsimd, nc.sync, nc.sync)):
+            queue.dma_start(
+                x_scale_table[32 * q : 32 * q + 4, :].bitcast(I32), x_scales[0, 4 * q : 4 * q + 4, :].bitcast(I32)
+            )
+        x_word_table = load_words("x_word_table", x_words, 4 * T)
+        sl_t = load_rows("sl_t", sl)
+        th_t = load_rows("th_t", th)
+        bias1 = minus_product("bias1", sl_t, th_t)
+        gs_t = load_rows("gs_t", gs)
+        sl2_t = load_rows("sl2_t", sl2)
+        th2_t = load_rows("th2_t", th2)
+        bias2 = minus_product("bias2", sl2_t, th2_t)
+
+        d_scale_picked = keep.tile([P, H], U8, name="d_scale_picked")
+        nc.vector.tensor_copy(d_scale_picked[:], d_scale_table[:].indirect(k1_t[:]))
+        d_scale_moved = keep.tile([P, H], U8, name="d_scale_moved")
+        nc.vector.tensor_copy(d_scale_moved[:].bitcast(I32), d_scale_picked[:].bitcast(I32))
+        for a in range(1, 4):
+            nc.scalar.dma_start(
+                d_scale_moved[a:P:32, :].bitcast(I32), d_scale_picked[8 * a : P : 32, :].bitcast(I32)
+            )
+        d_word_picked = keep.tile([P, H], U32, name="d_word_picked", tag="picked", align_bytes=64)
+        nc.vector.tensor_copy(d_word_picked[:], d_word_table[:].indirect(k1_t[:]))
+        d_word = keep.tile([P, H], U32, name="d_word", align_bytes=64)
+        nc.vector.tensor_copy(
+            d_word[:].rearrange("p (t m i) -> p m t i", t=PACK, i=4),
+            d_word_picked[:].rearrange("p (m i t) -> p m t i", t=PACK, i=4),
+        )
+        x_scale = keep.tile([P, S], U8, name="x_scale", tag="picked", align_bytes=64)
+        nc.vector.tensor_copy(x_scale[:], x_scale_table[:].indirect(offs_t[:]))
+        d_scale = keep.tile([P, H], U8, name="d_scale", align_bytes=64)
+        nc.vector.tensor_copy(
+            d_scale[:].rearrange("p (t m i) -> p m t i", t=PACK, i=16),
+            d_scale_moved[:].rearrange("p (m i t) -> p m t i", t=PACK, i=16),
+        )
+        x_word = keep.tile([P, S], U32, name="x_word", align_bytes=64)
+        nc.vector.tensor_copy(x_word[:], x_word_table[:].indirect(offs_t[:]))
+
+        mem_rows = mem.rearrange("(p t) u -> p t u", t=PACK)
+        out_rows = out.rearrange("(p t) u -> p t u", t=PACK)
+        page = []
+        for t in range(PACK):
+            tile = big.tile([P, U], F32, name=f"page{t}", offset=4 * U * t)
+            nc.sync.dma_start(tile[:], mem_rows[:, t, :])
+            page.append(tile)
+
+        def product(name, t, words, scales):
+            acc = psum.tile([P, S], F32, name=f"{name}_acc{t}")
+            cols = slice(P * t, P * (t + 1))
+            nc.tensor.matmul_mx(
+                out=acc[:],
+                lhsT=d_word[:, cols].bitcast(FP8X4),
+                lhsT_scale=d_scale[:, cols],
+                rhs=words[:].bitcast(FP8X4),
+                rhs_scale=scales[:],
+                start=True,
+                stop=True,
+            )
+            res = keep.tile([P, S], F32, name=f"{name}{t}")
+            nc.vector.tensor_scalar(res[:], acc[:], 0.0625, None, MULT)
+            return res
+
+        h = [product("h", t, x_word, x_scale) for t in range(PACK)]
+
+        ra = keep.tile([P, PACK, W], F32, name="ra", tag="ra_then_old")
+        rb = keep.tile([P, PACK, W], F32, name="rb")
+        dt = [keep.tile([P, S], F32, name=f"dt{t}") for t in range(PACK)]
+        z = keep.tile([P, S, PACK], BF16, name="z", align_bytes=64)
+
+        def pair_up(t):
+            fetched = keep.tile([P, 4, W], F32, name=f"fetched{t}")
+            sg2, pa, sg, pb = (fetched[:, i, :] for i in range(4))
+            scale, bias = sl_t[:, t : t + 1], bias1[:, t : t + 1]
+            nc.scalar.activation(sg2, h[t][:].indirect(n2_t[:]), SIGMOID, bias=bias, scale=scale)
+            nc.scalar.activation(pa, h[t][:].indirect(n1_t[:]), COPY)
+            nc.vector.tensor_tensor(ra[:, t, :], pa, sg2, MULT)
+            nc.scalar.activation(sg, h[t][:].indirect(n1_t[:]), SIGMOID, bias=bias, scale=scale)
+            nc.scalar.activation(pb, h[t][:].indirect(n2_t[:]), COPY)
+            nc.vector.tensor_tensor(rb[:, t, :], pb, sg, SUB)
+
+        def put_a(t):
+            nc.scalar.activation(dt[t][:].indirect(n1_t[:]), ra[:, t, :], COPY)
+
+        def put_b(t):
+            nc.scalar.activation(dt[t][:].indirect(n2_t[:]), rb[:, t, :], COPY)
+            nc.vector.tensor_scalar(z[:, :, t], dt[t][:], gs_t[:, t : t + 1], None, MULT)
+
+        for pair in ((0, 1), (2, 3)):
+            for t in pair:
+                pair_up(t)
+            for t in pair:
+                put_a(t)
+            for t in pair:
+                put_b(t)
+
+        z_word = keep.tile([P, S], U32, name="z_word", align_bytes=64)
+        z_scale = keep.tile([P, S], U8, name="z_scale", align_bytes=64)
+        nc.vector.quantize_mx(
+            out=z_word[:].bitcast(FP8X4), scales=z_scale[:], in_=z[:].rearrange("p j t -> p (j t)")
+        )
+
+        old = keep.tile([P, PACK, S], F32, name="old", tag="ra_then_old")
+        for t in range(PACK):
+            nc.scalar.activation(old[:, t, :], page[t][:].indirect(n3_t[:]), COPY)
+
+        h2 = [product("h2_", t, z_word, z_scale) for t in range(PACK)]
+
+        def blend(t):
+            sg3 = keep.tile([P, S], F32, name=f"sg3_{t}")
+            half = S // 2
+            for u in range(2):
+                nc.scalar.activation(
+                    sg3[:, half * u : half * (u + 1)],
+                    h2[t][:].indirect(n4_t[:, 8 * u : 8 * (u + 1)]),
+                    SIGMOID,
+                    bias=bias2[:, t : t + 1],
+                    scale=sl2_t[:, t : t + 1],
+                )
+            step = keep.tile([P, S], F32, name=f"step{t}")
+            nc.vector.tensor_tensor(step[:], h2[t][:], old[:, t, :], SUB)
+            gated = keep.tile([P, S], F32, name=f"gated{t}")
+            nc.vector.tensor_tensor(gated[:], step[:], sg3[:], MULT)
+            nw = keep.tile([P, S], F32, name=f"nw{t}")
+            nc.vector.tensor_tensor(nw[:], gated[:], old[:, t, :], ADD)
+            return nw
+
+        def put_back(t, nw):
+            nc.scalar.activation(page[t][:].indirect(n3_t[:]), nw[:], COPY)
+            nc.sync.dma_start(out_rows[:, t, :], page[t][:])
+
+        nws = [blend(0)]
+        for t in range(PACK):
+            if t + 1 < PACK:
+                nws.append(blend(t + 1))
+            put_back(t, nws[t])

@@ -20,6 +20,7 @@ SIGMOID = mybir.ActivationFunctionType.Sigmoid
 
 P = 128
 PACK = 4
+PAGE = 4 * U
 
 
 def tile_picked_ringeodepg_none_p_kernel(
@@ -37,10 +38,8 @@ def tile_picked_ringeodepg_none_p_kernel(
             nc.sync.dma_start(tile[:], src)
             return tile
 
-        def load_words(name, src, offset):
-            tile = big.tile([P, T], U32, name=name, offset=offset)
+        def load_words(tile, src):
             nc.sync.dma_start(tile[:].bitcast(I32), src[0].rearrange("p c r -> p (c r)").bitcast(I32))
-            return tile
 
         def load_rows(name, src):
             tile = keep.tile([P, PACK], F32, name=name)
@@ -54,25 +53,25 @@ def tile_picked_ringeodepg_none_p_kernel(
             nc.gpsimd.tensor_scalar(neg[:], prod[:], -1.0, 0.0, MULT, ADD)
             return neg
 
+        def load_scales(tile, src):
+            nc.sync.dma_start(
+                tile[:].bitcast(I32), src[0].bitcast(I32).unsqueeze(1).to_broadcast([16, 8, src.shape[2] // 4])
+            )
+
         k1_t = load_list("k1_t", k1)
         d_scale_table = keep.tile([P, G], U8, name="d_scale_table")
-        nc.sync.dma_start(
-            d_scale_table[:].bitcast(I32),
-            d_scales[0].bitcast(I32).unsqueeze(1).to_broadcast([16, 8, G // 4]),
-        )
+        load_scales(d_scale_table, d_scales)
         offs_t = load_list("offs_t", offs)
+        x_scale_table = keep.tile([P, T], U8, name="x_scale_table")
+        load_scales(x_scale_table, x_scales)
         n1_t = load_list("n1_t", n1)
         n2_t = load_list("n2_t", n2)
+        d_word_table = keep.tile([P, G], U32, name="d_word_table")
+        load_words(d_word_table, d_words)
+        x_word_table = big.tile([P, T], U32, name="x_word_table", offset=0)
+        load_words(x_word_table, x_words)
         n4_t = load_list("n4_t", n4)
-        d_word_table = load_words("d_word_table", d_words, 0)
         n3_t = load_list("n3_t", n3)
-        x_scale_table = keep.tile([P, T], U8, name="x_scale_table")
-        nc.vector.memset(x_scale_table[:].bitcast(I32), 0)
-        for q, queue in enumerate((nc.gpsimd, nc.gpsimd, nc.sync, nc.sync)):
-            queue.dma_start(
-                x_scale_table[32 * q : 32 * q + 4, :].bitcast(I32), x_scales[0, 4 * q : 4 * q + 4, :].bitcast(I32)
-            )
-        x_word_table = load_words("x_word_table", x_words, 4 * T)
         sl_t = load_rows("sl_t", sl)
         th_t = load_rows("th_t", th)
         bias1 = minus_product("bias1", sl_t, th_t)
@@ -83,34 +82,33 @@ def tile_picked_ringeodepg_none_p_kernel(
 
         d_scale_picked = keep.tile([P, H], U8, name="d_scale_picked")
         nc.vector.tensor_copy(d_scale_picked[:], d_scale_table[:].indirect(k1_t[:]))
-        d_scale_moved = keep.tile([P, H], U8, name="d_scale_moved")
-        nc.vector.tensor_copy(d_scale_moved[:].bitcast(I32), d_scale_picked[:].bitcast(I32))
+        joined = big.tile([P, H + S], U8, name="joined", offset=2 * PAGE)
+        nc.vector.tensor_copy(
+            joined[:, 0:H].rearrange("p (t m i) -> p m t i", t=PACK, i=16),
+            d_scale_picked[:].rearrange("p (m i t) -> p m t i", t=PACK, i=16),
+        )
+        x_scale_picked = keep.tile([P, S], U8, name="x_scale_picked")
+        nc.vector.tensor_copy(x_scale_picked[:], x_scale_table[:].indirect(offs_t[:]))
+        nc.vector.tensor_copy(joined[:, H : H + S].bitcast(I32), x_scale_picked[:].bitcast(I32))
+        placed = keep.tile([P, H + S], U8, name="placed", align_bytes=64)
+        nc.vector.tensor_copy(placed[:].bitcast(I32), joined[:].bitcast(I32))
         for a in range(1, 4):
-            nc.scalar.dma_start(
-                d_scale_moved[a:P:32, :].bitcast(I32), d_scale_picked[8 * a : P : 32, :].bitcast(I32)
-            )
-        d_word_picked = keep.tile([P, H], U32, name="d_word_picked", tag="picked", align_bytes=64)
+            nc.scalar.dma_start(placed[a:P:32, :].bitcast(I32), joined[8 * a : P : 32, :].bitcast(I32))
+        d_word_picked = big.tile([P, H], U32, name="d_word_picked", offset=3 * PAGE)
         nc.vector.tensor_copy(d_word_picked[:], d_word_table[:].indirect(k1_t[:]))
         d_word = keep.tile([P, H], U32, name="d_word", align_bytes=64)
         nc.vector.tensor_copy(
             d_word[:].rearrange("p (t m i) -> p m t i", t=PACK, i=4),
             d_word_picked[:].rearrange("p (m i t) -> p m t i", t=PACK, i=4),
         )
-        x_scale = keep.tile([P, S], U8, name="x_scale", tag="picked", align_bytes=64)
-        nc.vector.tensor_copy(x_scale[:], x_scale_table[:].indirect(offs_t[:]))
-        d_scale = keep.tile([P, H], U8, name="d_scale", align_bytes=64)
-        nc.vector.tensor_copy(
-            d_scale[:].rearrange("p (t m i) -> p m t i", t=PACK, i=16),
-            d_scale_moved[:].rearrange("p (m i t) -> p m t i", t=PACK, i=16),
-        )
-        x_word = keep.tile([P, S], U32, name="x_word", align_bytes=64)
+        x_word = big.tile([P, S], U32, name="x_word", offset=3 * PAGE, align_bytes=64)
         nc.vector.tensor_copy(x_word[:], x_word_table[:].indirect(offs_t[:]))
 
         mem_rows = mem.rearrange("(p t) u -> p t u", t=PACK)
         out_rows = out.rearrange("(p t) u -> p t u", t=PACK)
         page = []
         for t in range(PACK):
-            tile = big.tile([P, U], F32, name=f"page{t}", offset=4 * U * t)
+            tile = big.tile([P, U], F32, name=f"page{t}", offset=PAGE * t)
             nc.sync.dma_start(tile[:], mem_rows[:, t, :])
             page.append(tile)
 
@@ -120,9 +118,9 @@ def tile_picked_ringeodepg_none_p_kernel(
             nc.tensor.matmul_mx(
                 out=acc[:],
                 lhsT=d_word[:, cols].bitcast(FP8X4),
-                lhsT_scale=d_scale[:, cols],
+                lhsT_scale=placed[:, cols],
                 rhs=words[:].bitcast(FP8X4),
-                rhs_scale=scales[:],
+                rhs_scale=scales,
                 start=True,
                 stop=True,
             )
@@ -130,7 +128,7 @@ def tile_picked_ringeodepg_none_p_kernel(
             nc.vector.tensor_scalar(res[:], acc[:], 0.0625, None, MULT)
             return res
 
-        h = [product("h", t, x_word, x_scale) for t in range(PACK)]
+        h = [product("h", t, x_word, placed[:, H : H + S]) for t in range(PACK)]
 
         ra = keep.tile([P, PACK, W], F32, name="ra", tag="ra_then_old")
         rb = keep.tile([P, PACK, W], F32, name="rb")
@@ -173,7 +171,7 @@ def tile_picked_ringeodepg_none_p_kernel(
         for t in range(PACK):
             nc.scalar.activation(old[:, t, :], page[t][:].indirect(n3_t[:]), COPY)
 
-        h2 = [product("h2_", t, z_word, z_scale) for t in range(PACK)]
+        h2 = [product("h2_", t, z_word, z_scale[:]) for t in range(PACK)]
 
         def blend(t):
             sg3 = keep.tile([P, S], F32, name=f"sg3_{t}")

@@ -58,6 +58,11 @@ def tile_picked_ringeodepg_none_p_kernel(
                 tile[:].bitcast(I32), src[0].bitcast(I32).unsqueeze(1).to_broadcast([16, 8, src.shape[2] // 4])
             )
 
+        warm_in = keep.tile([P, 1], F32, name="warm_in")
+        nc.vector.memset(warm_in[:], 0.0)
+        warm_out = keep.tile([P, 1], F32, name="warm_out")
+        nc.scalar.activation(warm_out[:], warm_in[:], SIGMOID)
+
         k1_t = load_list("k1_t", k1)
         d_scale_table = keep.tile([P, G], U8, name="d_scale_table")
         load_scales(d_scale_table, d_scales)

@@ -31,6 +31,7 @@ def tile_picked_ringeodepg_none_p_kernel(
         lists = ctx.enter_context(tc.tile_pool(name="lists", bufs=1))
         keep = ctx.enter_context(tc.tile_pool(name="keep", bufs=1))
         big = ctx.enter_context(tc.tile_pool(name="big", bufs=1))
+        mid = ctx.enter_context(tc.tile_pool(name="mid", bufs=1))
         psum = ctx.enter_context(tc.psum_pool(name="psum", bufs=1))
 
         def load_list(name, src):
@@ -107,7 +108,9 @@ def tile_picked_ringeodepg_none_p_kernel(
             d_word_picked[:].rearrange("p (m i t) -> p m t i", t=PACK, i=4),
         )
         x_word = big.tile([P, S], U32, name="x_word", offset=3 * PAGE, align_bytes=64)
-        nc.vector.tensor_copy(x_word[:], x_word_table[:].indirect(offs_t[:]))
+        halves = (slice(0, S // 2), slice(S // 2, S))
+        for u, cols in enumerate(halves):
+            nc.vector.tensor_copy(x_word[:, cols], x_word_table[:].indirect(offs_t[:, 8 * u : 8 * (u + 1)]))
 
         mem_rows = mem.rearrange("(p t) u -> p t u", t=PACK)
         out_rows = out.rearrange("(p t) u -> p t u", t=PACK)
@@ -117,26 +120,29 @@ def tile_picked_ringeodepg_none_p_kernel(
             nc.sync.dma_start(tile[:], mem_rows[:, t, :])
             page.append(tile)
 
-        def product(name, t, words, scales):
-            acc = psum.tile([P, S], F32, name=f"{name}_acc{t}")
+        def product(acc, t, words, scales):
             cols = slice(P * t, P * (t + 1))
             nc.tensor.matmul_mx(
-                out=acc[:],
+                out=acc,
                 lhsT=d_word[:, cols].bitcast(FP8X4),
                 lhsT_scale=placed[:, cols],
-                rhs=words[:].bitcast(FP8X4),
+                rhs=words.bitcast(FP8X4),
                 rhs_scale=scales,
                 start=True,
                 stop=True,
             )
-            res = keep.tile([P, S], F32, name=f"{name}{t}")
-            nc.vector.tensor_scalar(res[:], acc[:], 0.0625, None, MULT)
-            return res
 
-        h = [product("h", t, x_word, placed[:, H : H + S]) for t in range(PACK)]
+        h = []
+        for t in range(PACK):
+            res = keep.tile([P, S], F32, name=f"h{t}")
+            for u, cols in enumerate(halves if t == 0 else (slice(0, S),)):
+                acc = psum.tile([P, cols.stop - cols.start], F32, name=f"bank{t + 4 * u}")
+                product(acc[:], t, x_word[:, cols], placed[:, H + cols.start : H + cols.stop])
+                nc.vector.tensor_scalar(res[:, cols], acc[:], 0.0625, None, MULT)
+            h.append(res)
 
-        ra = keep.tile([P, PACK, W], F32, name="ra", tag="ra_then_old")
-        rb = keep.tile([P, PACK, W], F32, name="rb")
+        ra = mid.tile([P, PACK, W], F32, name="ra", offset=1024)
+        rb = mid.tile([P, PACK, W], F32, name="rb", offset=5120)
         dt = [keep.tile([P, S], F32, name=f"dt{t}") for t in range(PACK)]
         z = keep.tile([P, S, PACK], BF16, name="z", align_bytes=64)
 
@@ -156,7 +162,8 @@ def tile_picked_ringeodepg_none_p_kernel(
 
         def put_b(t):
             nc.scalar.activation(dt[t][:].indirect(n2_t[:]), rb[:, t, :], COPY)
-            nc.vector.tensor_scalar(z[:, :, t], dt[t][:], gs_t[:, t : t + 1], None, MULT)
+            for cols in halves if t == PACK - 1 else (slice(0, S),):
+                nc.vector.tensor_scalar(z[:, cols, t], dt[t][:, cols], gs_t[:, t : t + 1], None, MULT)
 
         for pair in ((0, 1), (2, 3)):
             for t in pair:
@@ -168,33 +175,36 @@ def tile_picked_ringeodepg_none_p_kernel(
 
         z_word = keep.tile([P, S], U32, name="z_word", align_bytes=64)
         z_scale = keep.tile([P, S], U8, name="z_scale", align_bytes=64)
-        nc.vector.quantize_mx(
-            out=z_word[:].bitcast(FP8X4), scales=z_scale[:], in_=z[:].rearrange("p j t -> p (j t)")
-        )
+        for cols in halves:
+            nc.vector.quantize_mx(
+                out=z_word[:, cols].bitcast(FP8X4),
+                scales=z_scale[:, cols],
+                in_=z[:, cols, :].rearrange("p j t -> p (j t)"),
+            )
 
-        old = keep.tile([P, PACK, S], F32, name="old", tag="ra_then_old")
+        h2_old = [mid.tile([P, 2 * S], F32, name=f"h2_old{t}", offset=2048 * t) for t in range(PACK)]
+        h2 = [tile[:, 0:S] for tile in h2_old]
+        old = [tile[:, S : 2 * S] for tile in h2_old]
         for t in range(PACK):
-            nc.scalar.activation(old[:, t, :], page[t][:].indirect(n3_t[:]), COPY)
+            nc.scalar.activation(old[t], page[t][:].indirect(n3_t[:]), COPY)
 
-        h2 = [product("h2_", t, z_word, z_scale[:]) for t in range(PACK)]
+        for t in range(PACK):
+            acc = psum.tile([P, S], F32, name=f"bank{4 + t}")
+            for cols in halves:
+                product(acc[:, cols], t, z_word[:, cols], z_scale[:, cols])
+            nc.vector.tensor_scalar(h2[t], acc[:], 0.0625, None, MULT)
 
         def blend(t):
             sg3 = keep.tile([P, S], F32, name=f"sg3_{t}")
-            half = S // 2
-            for u in range(2):
-                nc.scalar.activation(
-                    sg3[:, half * u : half * (u + 1)],
-                    h2[t][:].indirect(n4_t[:, 8 * u : 8 * (u + 1)]),
-                    SIGMOID,
-                    bias=bias2[:, t : t + 1],
-                    scale=sl2_t[:, t : t + 1],
-                )
+            nc.scalar.activation(
+                sg3[:], h2_old[t][:].indirect(n4_t[:]), SIGMOID, bias=bias2[:, t : t + 1], scale=sl2_t[:, t : t + 1]
+            )
             step = keep.tile([P, S], F32, name=f"step{t}")
-            nc.vector.tensor_tensor(step[:], h2[t][:], old[:, t, :], SUB)
+            nc.vector.tensor_tensor(step[:], h2[t], old[t], SUB)
             gated = keep.tile([P, S], F32, name=f"gated{t}")
             nc.vector.tensor_tensor(gated[:], step[:], sg3[:], MULT)
             nw = keep.tile([P, S], F32, name=f"nw{t}")
-            nc.vector.tensor_tensor(nw[:], gated[:], old[:, t, :], ADD)
+            nc.vector.tensor_tensor(nw[:], gated[:], old[t], ADD)
             return nw
 
         def put_back(t, nw):

from contextlib import ExitStack

import concourse.mybir as mybir

K, T, S, G, H, W, U = 512, 2048, 256, 2048, 512, 128, 1024
FLOPS = 2 * 2 * K * H * S

F32 = mybir.dt.float32
BF16 = mybir.dt.bfloat16
I32 = mybir.dt.int32
U32 = mybir.dt.uint32
U16 = mybir.dt.uint16
U8 = mybir.dt.uint8
FP8X4 = mybir.dt.float8_e4m3fn_x4
MULT = mybir.AluOpType.mult
ADD = mybir.AluOpType.add
SUB = mybir.AluOpType.subtract
COPY = mybir.ActivationFunctionType.Copy
SIGMOID = mybir.ActivationFunctionType.Sigmoid

P = 128
PACK = 4
PAGE = 4 * U


def tile_picked_ringeodepg_none_p_kernel(
    tc, x_words, x_scales, d_words, d_scales, sl, th, gs, mem, sl2, th2, offs, k1, n1, n2, n3, n4, out
):
    nc = tc.nc
    with ExitStack() as ctx:
        lists = ctx.enter_context(tc.tile_pool(name="lists", bufs=1))
        keep = ctx.enter_context(tc.tile_pool(name="keep", bufs=1))
        big = ctx.enter_context(tc.tile_pool(name="big", bufs=1))
        mid = ctx.enter_context(tc.tile_pool(name="mid", bufs=1))
        psum = ctx.enter_context(tc.psum_pool(name="psum", bufs=1))

        def load_list(name, src):
            tile = lists.tile(list(src.shape), U16, name=name)
            nc.sync.dma_start(tile[:], src)
            return tile

        def load_words(tile, src):
            nc.sync.dma_start(tile[:].bitcast(I32), src[0].rearrange("p c r -> p (c r)").bitcast(I32))

        def load_rows(name, src):
            tile = keep.tile([P, PACK], F32, name=name)
            nc.gpsimd.dma_start(tile[:], src.rearrange("(p t) o -> p (t o)", t=PACK))
            return tile

        def minus_product(name, a, b):
            prod = keep.tile([P, PACK], F32, name=name + "_pos")
            nc.gpsimd.tensor_tensor(prod[:], a[:], b[:], MULT)
            neg = keep.tile([P, PACK], F32, name=name)
            nc.gpsimd.tensor_scalar(neg[:], prod[:], -1.0, 0.0, MULT, ADD)
            return neg

        def load_scales(tile, src):
            nc.sync.dma_start(
                tile[:].bitcast(I32), src[0].bitcast(I32).unsqueeze(1).to_broadcast([16, 8, src.shape[2] // 4])
            )

        warm_in = keep.tile([P, 1], F32, name="warm_in")
        nc.vector.memset(warm_in[:], 0.0)
        warm_out = keep.tile([P, 1], F32, name="warm_out")
        nc.scalar.activation(warm_out[:], warm_in[:], SIGMOID)

        k1_t = load_list("k1_t", k1)
        d_scale_table = keep.tile([P, G], U8, name="d_scale_table")
        load_scales(d_scale_table, d_scales)
        offs_t = load_list("offs_t", offs)
        x_scale_table = keep.tile([P, T], U8, name="x_scale_table")
        load_scales(x_scale_table, x_scales)
        n1_t = load_list("n1_t", n1)
        n2_t = load_list("n2_t", n2)
        d_word_table = keep.tile([P, G], U32, name="d_word_table")
        load_words(d_word_table, d_words)
        x_word_table = big.tile([P, T], U32, name="x_word_table", offset=0)
        load_words(x_word_table, x_words)
        n4_t = load_list("n4_t", n4)
        n3_t = load_list("n3_t", n3)
        sl_t = load_rows("sl_t", sl)
        th_t = load_rows("th_t", th)
        bias1 = minus_product("bias1", sl_t, th_t)
        gs_t = load_rows("gs_t", gs)
        sl2_t = load_rows("sl2_t", sl2)
        th2_t = load_rows("th2_t", th2)
        bias2 = minus_product("bias2", sl2_t, th2_t)

        d_scale_picked = keep.tile([P, H], U8, name="d_scale_picked")
        nc.vector.tensor_copy(d_scale_picked[:], d_scale_table[:].indirect(k1_t[:]))
        joined = big.tile([P, H + S], U8, name="joined", offset=2 * PAGE)
        nc.vector.tensor_copy(
            joined[:, 0:H].rearrange("p (t m i) -> p m t i", t=PACK, i=16),
            d_scale_picked[:].rearrange("p (m i t) -> p m t i", t=PACK, i=16),
        )
        x_scale_picked = keep.tile([P, S], U8, name="x_scale_picked")
        nc.vector.tensor_copy(x_scale_picked[:], x_scale_table[:].indirect(offs_t[:]))
        nc.vector.tensor_copy(joined[:, H : H + S].bitcast(I32), x_scale_picked[:].bitcast(I32))
        placed = keep.tile([P, H + S], U8, name="placed", align_bytes=64)
        nc.vector.tensor_copy(placed[:].bitcast(I32), joined[:].bitcast(I32))
        for a in range(1, 4):
            nc.scalar.dma_start(placed[a:P:32, :].bitcast(I32), joined[8 * a : P : 32, :].bitcast(I32))
        d_word_picked = big.tile([P, H], U32, name="d_word_picked", offset=3 * PAGE)
        nc.vector.tensor_copy(d_word_picked[:], d_word_table[:].indirect(k1_t[:]))
        d_word = keep.tile([P, H], U32, name="d_word", align_bytes=64)
        nc.vector.tensor_copy(
            d_word[:].rearrange("p (t m i) -> p m t i", t=PACK, i=4),
            d_word_picked[:].rearrange("p (m i t) -> p m t i", t=PACK, i=4),
        )
        x_word = big.tile([P, S], U32, name="x_word", offset=3 * PAGE, align_bytes=64)
        halves = (slice(0, S // 2), slice(S // 2, S))
        for u, cols in enumerate(halves):
            nc.vector.tensor_copy(x_word[:, cols], x_word_table[:].indirect(offs_t[:, 8 * u : 8 * (u + 1)]))

        mem_rows = mem.rearrange("(p t) u -> p t u", t=PACK)
        out_rows = out.rearrange("(p t) u -> p t u", t=PACK)
        page = []
        for t in range(PACK):
            tile = big.tile([P, U], F32, name=f"page{t}", offset=PAGE * t)
            nc.sync.dma_start(tile[:], mem_rows[:, t, :])
            page.append(tile)

        def product(acc, t, words, scales):
            cols = slice(P * t, P * (t + 1))
            nc.tensor.matmul_mx(
                out=acc,
                lhsT=d_word[:, cols].bitcast(FP8X4),
                lhsT_scale=placed[:, cols],
                rhs=words.bitcast(FP8X4),
                rhs_scale=scales,
                start=True,
                stop=True,
            )

        h = []
        for t in range(PACK):
            res = keep.tile([P, S], F32, name=f"h{t}")
            for u, cols in enumerate(halves if t == 0 else (slice(0, S),)):
                acc = psum.tile([P, cols.stop - cols.start], F32, name=f"bank{t + 4 * u}")
                product(acc[:], t, x_word[:, cols], placed[:, H + cols.start : H + cols.stop])
                nc.vector.tensor_scalar(res[:, cols], acc[:], 0.0625, None, MULT)
            h.append(res)

        ra = mid.tile([P, PACK, W], F32, name="ra", offset=1024)
        rb = mid.tile([P, PACK, W], F32, name="rb", offset=5120)
        dt = [keep.tile([P, S], F32, name=f"dt{t}") for t in range(PACK)]
        z = keep.tile([P, S, PACK], BF16, name="z", align_bytes=64)

        def pair_up(t):
            fetched = keep.tile([P, 4, W], F32, name=f"fetched{t}")
            sg2, pa, sg, pb = (fetched[:, i, :] for i in range(4))
            scale, bias = sl_t[:, t : t + 1], bias1[:, t : t + 1]
            nc.scalar.activation(sg2, h[t][:].indirect(n2_t[:]), SIGMOID, bias=bias, scale=scale)
            nc.scalar.activation(pa, h[t][:].indirect(n1_t[:]), COPY)
            nc.vector.tensor_tensor(ra[:, t, :], pa, sg2, MULT)
            nc.scalar.activation(sg, h[t][:].indirect(n1_t[:]), SIGMOID, bias=bias, scale=scale)
            nc.scalar.activation(pb, h[t][:].indirect(n2_t[:]), COPY)
            nc.vector.tensor_tensor(rb[:, t, :], pb, sg, SUB)

        def put_a(t):
            nc.scalar.activation(dt[t][:].indirect(n1_t[:]), ra[:, t, :], COPY)

        def put_b(t):
            nc.scalar.activation(dt[t][:].indirect(n2_t[:]), rb[:, t, :], COPY)
            for cols in halves if t == PACK - 1 else (slice(0, S),):
                nc.vector.tensor_scalar(z[:, cols, t], dt[t][:, cols], gs_t[:, t : t + 1], None, MULT)

        for pair in ((0, 1), (2, 3)):
            for t in pair:
                pair_up(t)
            for t in pair:
                put_a(t)
            for t in pair:
                put_b(t)

        z_word = keep.tile([P, S], U32, name="z_word", align_bytes=64)
        z_scale = keep.tile([P, S], U8, name="z_scale", align_bytes=64)
        for cols in halves:
            nc.vector.quantize_mx(
                out=z_word[:, cols].bitcast(FP8X4),
                scales=z_scale[:, cols],
                in_=z[:, cols, :].rearrange("p j t -> p (j t)"),
            )

        h2_old = [mid.tile([P, 2 * S], F32, name=f"h2_old{t}", offset=2048 * t) for t in range(PACK)]
        h2 = [tile[:, 0:S] for tile in h2_old]
        old = [tile[:, S : 2 * S] for tile in h2_old]
        for t in range(PACK):
            nc.scalar.activation(old[t], page[t][:].indirect(n3_t[:]), COPY)

        for t in range(PACK):
            acc = psum.tile([P, S], F32, name=f"bank{4 + t}")
            for cols in halves:
                product(acc[:, cols], t, z_word[:, cols], z_scale[:, cols])
            nc.vector.tensor_scalar(h2[t], acc[:], 0.0625, None, MULT)

        def blend(t):
            sg3 = keep.tile([P, S], F32, name=f"sg3_{t}")
            nc.scalar.activation(
                sg3[:], h2_old[t][:].indirect(n4_t[:]), SIGMOID, bias=bias2[:, t : t + 1], scale=sl2_t[:, t : t + 1]
            )
            step = keep.tile([P, S], F32, name=f"step{t}")
            nc.vector.tensor_tensor(step[:], h2[t], old[t], SUB)
            gated = keep.tile([P, S], F32, name=f"gated{t}")
            nc.vector.tensor_tensor(gated[:], step[:], sg3[:], MULT)
            nw = keep.tile([P, S], F32, name=f"nw{t}")
            nc.vector.tensor_tensor(nw[:], gated[:], old[t], ADD)
            return nw

        def put_back(t, nw):
            nc.scalar.activation(page[t][:].indirect(n3_t[:]), nw[:], COPY)
            nc.sync.dma_start(out_rows[:, t, :], page[t][:])

        nws = [blend(0)]
        for t in range(PACK):
            if t + 1 < PACK:
                nws.append(blend(t + 1))
            put_back(t, nws[t])
